import numpy as np, ml_dtypes
CORES = [102,230,358,486]
N = 4
ROOT = 0
def setup_inputs(rng):
    return {"x": rng.standard_normal((N, 128, N * 512), dtype=np.float32).astype(ml_dtypes.bfloat16)}
def reference(x):
    return {"y": np.stack([x[ROOT][:, r * 512:(r + 1) * 512] for r in range(N)])}

@@ -1,0 +1,53 @@
+import concourse.bass as bass
+
+SCRATCH = {
+    "a": ("dram", [128, 512], "bfloat16"),
+    "b": ("dram", [128, 512], "bfloat16"),
+    "c": ("dram", [2, 128, 256], "bfloat16"),
+}
+SEMAPHORES = ["ld_a", "ld_b", "ld_c", "st", "sent", "got", "got_c"]
+
+LO, HI, ALL8 = 0x0F, 0xF0, 0xFF
+
+
+def rank_program(g, core, T, topo):
+    root, r1, r2, r3 = T.cores
+    relays = {r1 + 1: 0, r3 + 1: 1}
+    S = T.sem
+
+    def to(d):
+        rid, pid = topo.addr(d, core)
+        return bass.DstId(rid=rid, pnc=pid)
+
+    if core == root:
+        g.dma_start(T.c[:], T.x[:, 1024:1536]).then_inc(S.ld_c, 16)
+        g.dma_start(T.a[:], T.x[:, 512:1024]).then_inc(S.ld_a, 16)
+        g.dma_start(T.b[:], T.x[:, 1536:2048]).then_inc(S.ld_b, 16)
+        g.wait_ge(S.ld_c, 16)
+        g.remote_dma_fused([
+            bass.RemoteDMATransfer(dst_ids=[to(r1 + 1)], dma_engine_mask=LO, remote_sem=S.got_c, src=T.c[0], dst=T.c[0]),
+            bass.RemoteDMATransfer(dst_ids=[to(r3 + 1)], dma_engine_mask=HI, remote_sem=S.got_c, src=T.c[1], dst=T.c[1]),
+        ], local_sem=S.sent)
+        g.wait_ge(S.ld_a, 16)
+        g.wait_ge(S.ld_b, 16)
+        g.remote_dma_fused([
+            bass.RemoteDMATransfer(dst_ids=[to(r1)], dma_engine_mask=LO, remote_sem=S.got, src=T.a[:], dst=T.a[:]),
+            bass.RemoteDMATransfer(dst_ids=[to(r3)], dma_engine_mask=HI, remote_sem=S.got, src=T.b[:], dst=T.a[:]),
+        ], local_sem=S.sent)
+        g.dma_start(T.y[:], T.x[:, 0:512]).then_inc(S.st, 16)
+        g.wait_ge(S.sent, 16)
+        g.wait_ge(S.st, 16)
+    elif core in relays:
+        h = relays[core]
+        rid, pid = topo.addr(r2, core)
+        g.wait_ge(S.got_c, 4)
+        g.remote_dma(T.c[h], T.c[h], S.got_c, S.sent, pid, rid, ALL8)
+        g.wait_ge(S.sent, 8)
+    elif core == r2:
+        g.wait_ge(S.got_c, 16)
+        g.dma_start(T.y[:], T.c[:]).then_inc(S.st, 16)
+        g.wait_ge(S.st, 16)
+    elif core in (r1, r3):
+        g.wait_ge(S.got, 4)
+        g.dma_start(T.y[:], T.a[:]).then_inc(S.st, 16)
+        g.wait_ge(S.st, 16)

@@ -3,7 +3,7 @@ import concourse.bass as bass
 SCRATCH = {
     "a": ("dram", [128, 512], "bfloat16"),
     "b": ("dram", [128, 512], "bfloat16"),
-    "c": ("dram", [2, 128, 256], "bfloat16"),
+    "c": ("dram", [4, 128, 128], "bfloat16"),
 }
 SEMAPHORES = ["ld_a", "ld_b", "ld_c", "st", "sent", "got", "got_c"]
 
@@ -12,7 +12,8 @@ LO, HI, ALL8 = 0x0F, 0xF0, 0xFF
 
 def rank_program(g, core, T, topo):
     root, r1, r2, r3 = T.cores
-    relays = {r1 + 1: 0, r3 + 1: 1}
+    chip12 = r1 - r1 % 8
+    relays = [chip12 + 0, chip12 + 4, chip12 + 8 + 2, chip12 + 8 + 6]
     S = T.sem
 
     def to(d):
@@ -21,15 +22,16 @@ def rank_program(g, core, T, topo):
 
     if core == root:
         g.dma_start(T.c[:], T.x[:, 1024:1536]).then_inc(S.ld_c, 16)
-        g.dma_start(T.a[:], T.x[:, 512:1024]).then_inc(S.ld_a, 16)
         g.dma_start(T.b[:], T.x[:, 1536:2048]).then_inc(S.ld_b, 16)
+        g.dma_start(T.a[:], T.x[:, 512:1024]).then_inc(S.ld_a, 16)
         g.wait_ge(S.ld_c, 16)
         g.remote_dma_fused([
-            bass.RemoteDMATransfer(dst_ids=[to(r1 + 1)], dma_engine_mask=LO, remote_sem=S.got_c, src=T.c[0], dst=T.c[0]),
-            bass.RemoteDMATransfer(dst_ids=[to(r3 + 1)], dma_engine_mask=HI, remote_sem=S.got_c, src=T.c[1], dst=T.c[1]),
+            bass.RemoteDMATransfer(dst_ids=[to(rl)], dma_engine_mask=0x3 << (2 * q), remote_sem=S.got_c,
+                                   src=T.c[q], dst=T.c[q])
+            for q, rl in enumerate(relays)
         ], local_sem=S.sent)
-        g.wait_ge(S.ld_a, 16)
         g.wait_ge(S.ld_b, 16)
+        g.wait_ge(S.ld_a, 16)
         g.remote_dma_fused([
             bass.RemoteDMATransfer(dst_ids=[to(r1)], dma_engine_mask=LO, remote_sem=S.got, src=T.a[:], dst=T.a[:]),
             bass.RemoteDMATransfer(dst_ids=[to(r3)], dma_engine_mask=HI, remote_sem=S.got, src=T.b[:], dst=T.a[:]),
@@ -38,13 +40,13 @@ def rank_program(g, core, T, topo):
         g.wait_ge(S.sent, 16)
         g.wait_ge(S.st, 16)
     elif core in relays:
-        h = relays[core]
+        q = relays.index(core)
         rid, pid = topo.addr(r2, core)
-        g.wait_ge(S.got_c, 4)
-        g.remote_dma(T.c[h], T.c[h], S.got_c, S.sent, pid, rid, ALL8)
+        g.wait_ge(S.got_c, 2)
+        g.remote_dma(T.c[q], T.c[q], S.got_c, S.sent, pid, rid, ALL8)
         g.wait_ge(S.sent, 8)
     elif core == r2:
-        g.wait_ge(S.got_c, 16)
+        g.wait_ge(S.got_c, 32)
         g.dma_start(T.y[:], T.c[:]).then_inc(S.st, 16)
         g.wait_ge(S.st, 16)
     elif core in (r1, r3):

@@ -2,18 +2,20 @@ import concourse.bass as bass
 
 SCRATCH = {
     "a": ("dram", [128, 512], "bfloat16"),
-    "b": ("dram", [128, 512], "bfloat16"),
+    "b": ("dram", [4, 128, 128], "bfloat16"),
     "c": ("dram", [4, 128, 128], "bfloat16"),
 }
-SEMAPHORES = ["ld_a", "ld_b", "ld_c", "st", "sent", "got", "got_c"]
+SEMAPHORES = ["ld_a", "ld_b", "ld_c", "st", "sent", "got"]
 
-LO, HI, ALL8 = 0x0F, 0xF0, 0xFF
+ALL8 = 0xFF
 
 
 def rank_program(g, core, T, topo):
     root, r1, r2, r3 = T.cores
-    chip12 = r1 - r1 % 8
-    relays = [chip12 + 0, chip12 + 4, chip12 + 8 + 2, chip12 + 8 + 6]
+    chip_h1 = r1 - r1 % 8
+    chip_h0 = root - root % 8
+    relays = [chip_h1 + 0, chip_h1 + 4, chip_h1 + 8 + 2, chip_h1 + 8 + 6]
+    helpers = [None, chip_h0 + 0, chip_h0 + 2, chip_h0 + 4]
     S = T.sem
 
     def to(d):
@@ -26,30 +28,41 @@ def rank_program(g, core, T, topo):
         g.dma_start(T.a[:], T.x[:, 512:1024]).then_inc(S.ld_a, 16)
         g.wait_ge(S.ld_c, 16)
         g.remote_dma_fused([
-            bass.RemoteDMATransfer(dst_ids=[to(rl)], dma_engine_mask=0x3 << (2 * q), remote_sem=S.got_c,
+            bass.RemoteDMATransfer(dst_ids=[to(rl)], dma_engine_mask=0x3 << (2 * q), remote_sem=S.got,
                                    src=T.c[q], dst=T.c[q])
             for q, rl in enumerate(relays)
         ], local_sem=S.sent)
         g.wait_ge(S.ld_b, 16)
+        g.remote_dma_fused(
+            [bass.RemoteDMATransfer(dst_ids=[to(r3)], dma_engine_mask=0xF0, remote_sem=S.got,
+                                    src=T.b[0], dst=T.b[0])] +
+            [bass.RemoteDMATransfer(dst_ids=[to(helpers[q])], dma_engine_mask=0x3 << (6 + 2 * q), remote_sem=S.got,
+                                    src=T.b[q], dst=T.b[q]) for q in (1, 2, 3)],
+            local_sem=S.sent)
         g.wait_ge(S.ld_a, 16)
-        g.remote_dma_fused([
-            bass.RemoteDMATransfer(dst_ids=[to(r1)], dma_engine_mask=LO, remote_sem=S.got, src=T.a[:], dst=T.a[:]),
-            bass.RemoteDMATransfer(dst_ids=[to(r3)], dma_engine_mask=HI, remote_sem=S.got, src=T.b[:], dst=T.a[:]),
-        ], local_sem=S.sent)
+        rid, pid = topo.addr(r1, core)
+        g.remote_dma(T.a[:], T.a[:], S.got, S.sent, pid, rid, 0x0F)
         g.dma_start(T.y[:], T.x[:, 0:512]).then_inc(S.st, 16)
-        g.wait_ge(S.sent, 16)
+        g.wait_ge(S.sent, 22)
         g.wait_ge(S.st, 16)
-    elif core in relays:
-        q = relays.index(core)
-        rid, pid = topo.addr(r2, core)
-        g.wait_ge(S.got_c, 2)
-        g.remote_dma(T.c[q], T.c[q], S.got_c, S.sent, pid, rid, ALL8)
+    elif core in relays or core in helpers:
+        if core in relays:
+            buf, q, d = T.c, relays.index(core), r2
+        else:
+            buf, q, d = T.b, helpers.index(core), r3
+        rid, pid = topo.addr(d, core)
+        g.wait_ge(S.got, 2)
+        g.remote_dma(buf[q], buf[q], S.got, S.sent, pid, rid, ALL8)
         g.wait_ge(S.sent, 8)
     elif core == r2:
-        g.wait_ge(S.got_c, 32)
+        g.wait_ge(S.got, 32)
         g.dma_start(T.y[:], T.c[:]).then_inc(S.st, 16)
         g.wait_ge(S.st, 16)
-    elif core in (r1, r3):
+    elif core == r3:
+        g.wait_ge(S.got, 28)
+        g.dma_start(T.y[:], T.b[:]).then_inc(S.st, 16)
+        g.wait_ge(S.st, 16)
+    elif core == r1:
         g.wait_ge(S.got, 4)
         g.dma_start(T.y[:], T.a[:]).then_inc(S.st, 16)
         g.wait_ge(S.st, 16)

@@ -14,7 +14,7 @@ def rank_program(g, core, T, topo):
     root, r1, r2, r3 = T.cores
     chip_h1 = r1 - r1 % 8
     chip_h0 = root - root % 8
-    relays = [chip_h1 + 0, chip_h1 + 4, chip_h1 + 8 + 2, chip_h1 + 8 + 6]
+    relays = [chip_h1 + 0, chip_h1 + 4, chip_h1 + 2, chip_h1 + 7]
     helpers = [None, chip_h0 + 0, chip_h0 + 2, chip_h0 + 4]
     S = T.sem
 
@@ -41,9 +41,9 @@ def rank_program(g, core, T, topo):
             local_sem=S.sent)
         g.wait_ge(S.ld_a, 16)
         rid, pid = topo.addr(r1, core)
-        g.remote_dma(T.a[:], T.a[:], S.got, S.sent, pid, rid, 0x0F)
+        g.remote_dma(T.a[:], T.a[:], S.got, S.sent, pid, rid, ALL8)
         g.dma_start(T.y[:], T.x[:, 0:512]).then_inc(S.st, 16)
-        g.wait_ge(S.sent, 22)
+        g.wait_ge(S.sent, 26)
         g.wait_ge(S.st, 16)
     elif core in relays or core in helpers:
         if core in relays:
@@ -54,15 +54,8 @@ def rank_program(g, core, T, topo):
         g.wait_ge(S.got, 2)
         g.remote_dma(buf[q], buf[q], S.got, S.sent, pid, rid, ALL8)
         g.wait_ge(S.sent, 8)
-    elif core == r2:
-        g.wait_ge(S.got, 32)
-        g.dma_start(T.y[:], T.c[:]).then_inc(S.st, 16)
-        g.wait_ge(S.st, 16)
-    elif core == r3:
-        g.wait_ge(S.got, 28)
-        g.dma_start(T.y[:], T.b[:]).then_inc(S.st, 16)
-        g.wait_ge(S.st, 16)
-    elif core == r1:
-        g.wait_ge(S.got, 4)
-        g.dma_start(T.y[:], T.a[:]).then_inc(S.st, 16)
+    elif core in (r1, r2, r3):
+        buf, n = {r1: (T.a, 8), r2: (T.c, 32), r3: (T.b, 28)}[core]
+        g.wait_ge(S.got, n)
+        g.dma_start(T.y[:], buf[:]).then_inc(S.st, 16)
         g.wait_ge(S.st, 16)

import concourse.bass as bass

SCRATCH = {
    "a": ("dram", [128, 512], "bfloat16"),
    "b": ("dram", [4, 128, 128], "bfloat16"),
    "c": ("dram", [4, 128, 128], "bfloat16"),
}
SEMAPHORES = ["ld_a", "ld_b", "ld_c", "st", "sent", "got"]

ALL8 = 0xFF


def rank_program(g, core, T, topo):
    root, r1, r2, r3 = T.cores
    chip_h1 = r1 - r1 % 8
    chip_h0 = root - root % 8
    relays = [chip_h1 + 0, chip_h1 + 4, chip_h1 + 2, chip_h1 + 7]
    helpers = [None, chip_h0 + 0, chip_h0 + 2, chip_h0 + 4]
    S = T.sem

    def to(d):
        rid, pid = topo.addr(d, core)
        return bass.DstId(rid=rid, pnc=pid)

    if core == root:
        g.dma_start(T.c[:], T.x[:, 1024:1536]).then_inc(S.ld_c, 16)
        g.dma_start(T.b[:], T.x[:, 1536:2048]).then_inc(S.ld_b, 16)
        g.dma_start(T.a[:], T.x[:, 512:1024]).then_inc(S.ld_a, 16)
        g.wait_ge(S.ld_c, 16)
        g.remote_dma_fused([
            bass.RemoteDMATransfer(dst_ids=[to(rl)], dma_engine_mask=0x3 << (2 * q), remote_sem=S.got,
                                   src=T.c[q], dst=T.c[q])
            for q, rl in enumerate(relays)
        ], local_sem=S.sent)
        g.wait_ge(S.ld_b, 16)
        g.remote_dma_fused(
            [bass.RemoteDMATransfer(dst_ids=[to(r3)], dma_engine_mask=0xF0, remote_sem=S.got,
                                    src=T.b[0], dst=T.b[0])] +
            [bass.RemoteDMATransfer(dst_ids=[to(helpers[q])], dma_engine_mask=0x3 << (6 + 2 * q), remote_sem=S.got,
                                    src=T.b[q], dst=T.b[q]) for q in (1, 2, 3)],
            local_sem=S.sent)
        g.wait_ge(S.ld_a, 16)
        rid, pid = topo.addr(r1, core)
        g.remote_dma(T.a[:], T.a[:], S.got, S.sent, pid, rid, ALL8)
        g.dma_start(T.y[:], T.x[:, 0:512]).then_inc(S.st, 16)
        g.wait_ge(S.sent, 26)
        g.wait_ge(S.st, 16)
    elif core in relays or core in helpers:
        if core in relays:
            buf, q, d = T.c, relays.index(core), r2
        else:
            buf, q, d = T.b, helpers.index(core), r3
        rid, pid = topo.addr(d, core)
        g.wait_ge(S.got, 2)
        g.remote_dma(buf[q], buf[q], S.got, S.sent, pid, rid, ALL8)
        g.wait_ge(S.sent, 8)
    elif core in (r1, r2, r3):
        buf, n = {r1: (T.a, 8), r2: (T.c, 32), r3: (T.b, 28)}[core]
        g.wait_ge(S.got, n)
        g.dma_start(T.y[:], buf[:]).then_inc(S.st, 16)
        g.wait_ge(S.st, 16)
